import numpy as np
import ml_dtypes


def mxq(x, axis, fmt="e4m3"):
    dtype, down = {"e4m3": (ml_dtypes.float8_e4m3fn, 7), "e5m2": (ml_dtypes.float8_e5m2, 14)}[fmt]
    v = np.moveaxis(np.asarray(x, np.float32).astype(ml_dtypes.bfloat16).astype(np.float64), axis, -1)
    blocks = v.reshape(v.shape[:-1] + (-1, 32))
    amax = np.abs(blocks).max(-1, keepdims=True)
    byte = np.maximum(np.where(amax > 0, np.frexp(amax)[1] - 1 + 127, 0) - down, 1)
    scale = np.exp2(byte - 127.0)
    codes = (blocks / scale).astype(np.float32).astype(dtype).astype(np.float64)
    return np.moveaxis((codes * scale).reshape(v.shape), -1, axis)


WIDE = False


def mx_kscale(k, group=512):
    if not WIDE:
        return np.ones(k)
    levels = np.array([10, -10, 5, -5, 0])
    if group != 512:
        return np.exp2(np.random.permutation(np.resize(levels, k // group))).repeat(group)
    if k % 512:
        return np.exp2(np.random.permutation(np.resize(levels, k // 32))).repeat(32)
    a = np.empty((k // 512, 16))
    for p in range(k // 512):
        a[p, :8] = np.random.permutation(np.resize(levels, 8))
        for g in range(8):
            far = levels[np.abs(levels - a[p, g]) >= 10]
            a[p, g + 8] = far[np.random.randint(len(far))]
    return np.exp2(a.ravel()).repeat(32)


def f64(x):
    return np.asarray(x).astype(np.float64)


def striped(idx):
    return np.tile(np.asarray(idx).reshape(-1, 16).T, (8, 1)).astype(np.uint16)


def unstriped(offs):
    return offs[:16].T.reshape(-1).astype(np.int64)


H, KV, D, NQ, N = 8, 2, 128, 512, 512


def setup_inputs():
    n = np.random.standard_normal
    s = mx_kscale(D, 0)[:, None]
    u = mx_kscale(N)
    t = np.random.uniform(0.5, 2.0, N) * u
    v = n((KV, N, 128))
    return {
        "qT": (n((H, D, NQ)) * s * (0.70 / np.sqrt(D))).astype(np.float32),
        "kT": (n((KV, D, N)) / s).astype(np.float32),
        "t": t.reshape(N, 1).astype(np.float32),
        "v": (v / t[:, None]).astype(np.float32),
        "gn": np.tile(np.random.uniform(0.5, 2.0, 128), (128, 1)).astype(np.float32),
    }


def reference(qT, kT, t, v, gn):
    a = np.repeat(mxq(f64(kT), 1, "e4m3"), H // KV, 0).transpose(0, 2, 1) @ mxq(f64(qT), 1, "e4m3")
    p = np.tanh(a)
    w = p * f64(t)
    y = mxq(w, 1, "e4m3").transpose(0, 2, 1) @ np.repeat(mxq(f64(v), 1, "e4m3"), H // KV, 0)
    y = y / 16.0
    y = y / np.sqrt(np.mean(np.square(y), -1, keepdims=True) + 1e-5) * f64(gn)[:1]
    return y

@@ -1,0 +1,198 @@
+from contextlib import ExitStack
+
+import concourse.mybir as mybir
+
+H, KV, D, NQ, N = 8, 2, 128, 512, 512
+FLOPS = 2 * 2 * H * NQ * N * D
+
+F32 = mybir.dt.float32
+BF16 = mybir.dt.bfloat16
+U32 = mybir.dt.uint32
+U8 = mybir.dt.uint8
+FP8X4 = mybir.dt.float8_e4m3fn_x4
+ACT = mybir.ActivationFunctionType
+MULT = mybir.AluOpType.mult
+
+P = 128
+PACK = 4
+ROWS = 32
+TILES = 4
+COLS = 128
+SETS = 2
+PAIRS = 16
+EPS = 1e-5
+
+
+def head_of(s, g):
+    return 4 * (g // 2) + 2 * s + g % 2
+
+
+def deal(copy, dealt, raw, places, part):
+    run = PACK // places
+    src = raw.rearrange("p j (a b r) -> p a j b r", b=run, r=places)
+    dst = dealt.rearrange("p (r a b j) -> p a j b r", r=places, b=run, j=PACK)
+    rows = slice(part.start // run, part.stop // run)
+    copy(out=dst[:, rows], in_=src[:, rows])
+
+
+def tile_rows_a_tanh_onorm_kernel(tc, qT, kT, t, v, gn, out):
+    nc = tc.nc
+    with ExitStack() as ctx:
+        sb = ctx.enter_context(tc.tile_pool(name="sb", bufs=1))
+        ps = ctx.enter_context(tc.psum_pool(name="ps", bufs=1))
+        ctx.enter_context(tc.manual_schedule())
+
+        def mx_tiles(name, words):
+            values = sb.tile([P, PACK * words], BF16, name=name + "_bf", align_bytes=64)
+            codes = sb.tile([P, words], U32, name=name + "_codes", align_bytes=64)
+            scales = sb.tile([P, words], U8, name=name + "_scales", align_bytes=64)
+            return values, codes, scales
+
+        def quantize(tiles):
+            values, codes, scales = tiles
+            nc.vector.quantize_mx(out=codes[:].bitcast(FP8X4), scales=scales[:], in_=values[:])
+
+        chunks = [(0, 0, 256), (0, 256, 256), (1, 0, 512)]
+
+        k_raw = sb.tile([P, PACK, N], F32, name="k_raw", align_bytes=64)
+        q_raw = [sb.tile([P, PACK, c[2]], F32, name="q_raw%d" % i, align_bytes=64) for i, c in enumerate(chunks)]
+        v_raw = sb.tile([P, KV, PACK * D], F32, name="v_raw", align_bytes=64)
+        t_sb = sb.tile([P, PACK], F32, name="t_sb", align_bytes=64)
+        gn_sb = sb.tile([P, D], F32, name="gn_sb", align_bytes=64)
+        queues = [nc.sync, nc.scalar]
+
+        for dup in range(2):
+            for kv in range(KV):
+                g = 2 * kv + dup
+                queues[kv].dma_start(out=k_raw[ROWS * g : ROWS * (g + 1)], in_=kT[kv].rearrange("(p j) n -> p j n", j=PACK))
+
+        def load_q(i):
+            s, q0, width = chunks[i]
+            for kv in range(KV):
+                h0 = head_of(s, 2 * kv)
+                src = qT[h0 : h0 + 2].rearrange("h (p j) q -> (h p) j q", j=PACK)
+                queues[kv].dma_start(out=q_raw[i][64 * kv : 64 * (kv + 1)], in_=src[:, :, q0 : q0 + width])
+
+        load_q(0)
+        load_q(1)
+        nc.sync.dma_start(out=t_sb[:], in_=t.rearrange("(p r) o -> p (r o)", r=PACK))
+        nc.sync.dma_start(out=v_raw[:], in_=v.rearrange("k (p r) e -> p k (r e)", r=PACK))
+        load_q(2)
+        nc.sync.dma_start(out=gn_sb[:], in_=gn)
+
+        k_mx = mx_tiles("k", N)
+        q_mx = [mx_tiles("q%d" % i, c[2]) for i, c in enumerate(chunks)]
+        v_mx = mx_tiles("v", KV * D)
+        w_mx = [mx_tiles("w%d" % j, 2 * COLS) for j in range(PAIRS)]
+        p_sb = [sb.tile([P, 2, COLS, PACK], F32, name="p%d" % j, align_bytes=64) for j in range(PAIRS)]
+        scores = [ps.tile([P, PACK * COLS], F32, name="scores%d" % g) for g in range(TILES)]
+        y = [ps.tile([P, PACK * D], F32, name="y%d" % g) for g in range(TILES)]
+        ssq = sb.tile([P, SETS * TILES, 8], F32, name="ssq", align_bytes=64)
+        rstd = sb.tile([P, SETS * TILES, 8], F32, name="rstd", align_bytes=64)
+        squares = [sb.tile([P, PACK * D], F32, name="squares%d" % i, align_bytes=64) for i in range(2)]
+        result = [sb.tile([P, PACK, D], F32, name="result%d" % i, align_bytes=64) for i in range(SETS * TILES)]
+
+        def score_matmuls(j):
+            s, tau, half = j // 8, (j % 8) // 2, j % 2
+            if s == 0:
+                codes, scales = q_mx[tau // 2][1:]
+                qc = slice(COLS * (tau % 2), COLS * (tau % 2 + 1))
+            else:
+                codes, scales = q_mx[2][1:]
+                qc = slice(COLS * tau, COLS * (tau + 1))
+            for r in range(PACK):
+                kc = slice(COLS * r, COLS * (r + 1))
+                for g in (2 * half, 2 * half + 1):
+                    rows = slice(ROWS * g, ROWS * (g + 1))
+                    nc.tensor.matmul_mx(
+                        out=scores[g][:, kc],
+                        lhsT=k_mx[1][rows, kc].bitcast(FP8X4), lhsT_scale=k_mx[2][rows, kc],
+                        rhs=codes[rows, qc].bitcast(FP8X4), rhs_scale=scales[rows, qc],
+                        start=True, stop=True,
+                    )
+
+        def tanh(j):
+            for i in range(2):
+                g = 2 * (j % 2) + i
+                nc.scalar.activation(
+                    out=p_sb[j][:, i], in_=scores[g][:].rearrange("p (r n) -> p n r", r=PACK), func=ACT.Tanh
+                )
+
+        def weigh(j):
+            nc.vector.tensor_tensor(
+                out=w_mx[j][0][:].rearrange("p (n r) -> p n r", r=PACK),
+                in0=p_sb[j][:].rearrange("p i n r -> p (i n) r"),
+                in1=t_sb[:].unsqueeze(1).to_broadcast([P, 2 * COLS, PACK]),
+                op=MULT,
+            )
+
+        def value_matmuls(s, g):
+            vc = slice(D * (g // 2), D * (g // 2 + 1))
+            wc = slice(COLS * (g % 2), COLS * (g % 2 + 1))
+            for tau in range(PACK):
+                codes, scales = w_mx[8 * s + 2 * tau + g // 2][1:]
+                nc.tensor.matmul_mx(
+                    out=y[g][:, D * tau : D * (tau + 1)],
+                    lhsT=codes[:, wc].bitcast(FP8X4), lhsT_scale=scales[:, wc],
+                    rhs=v_mx[1][:, vc].bitcast(FP8X4), rhs_scale=v_mx[2][:, vc],
+                    start=True, stop=True,
+                )
+
+        def norm(s, g):
+            u = TILES * s + g
+            for tau in range(PACK):
+                cols = slice(D * tau, D * (tau + 1))
+                nc.scalar.activation(
+                    out=squares[u % 2][:, cols], in_=y[g][:, cols], func=ACT.Square, scale=1.0 / 16,
+                    accum_out=ssq[:, u, tau : tau + 1],
+                )
+            nc.scalar.activation(
+                out=rstd[:, u, 0:PACK], in_=ssq[:, u, 0:PACK], func=ACT.Abs_reciprocal_sqrt,
+                scale=256.0 / D, bias=256.0 * EPS,
+            )
+
+        def finish(s, g):
+            u = TILES * s + g
+            for tau in range(PACK):
+                nc.vector.scalar_tensor_tensor(
+                    out=result[u][:, tau], in0=y[g][:, D * tau : D * (tau + 1)], scalar=rstd[:, u, tau : tau + 1],
+                    in1=gn_sb[:], op0=MULT, op1=MULT,
+                )
+            nchunks = 2 if s == 0 else 1
+            dst = out[head_of(s, g)].rearrange("(c p r) e -> p c (r e)", c=nchunks, p=P)
+            nc.sync.dma_start(out=dst, in_=result[u][:].rearrange("p (c r) e -> p c (r e)", c=nchunks))
+
+        deal(nc.vector.tensor_copy, k_mx[0][:], k_raw[:], 4, slice(0, COLS))
+        quantize(k_mx)
+        deal(nc.scalar.copy, q_mx[0][0][:], q_raw[0][:], 2, slice(0, COLS))
+        quantize(q_mx[0])
+        score_matmuls(0)
+        score_matmuls(1)
+        deal(nc.vector.tensor_copy, q_mx[1][0][:], q_raw[1][:], 2, slice(0, COLS))
+        nc.vector.tensor_copy(
+            out=v_mx[0][:].rearrange("p (k c i r) -> p k c r i", k=KV, i=4, r=PACK),
+            in_=v_raw[:].rearrange("p k (r c i) -> p k c r i", r=PACK, i=4),
+        )
+        quantize(q_mx[1])
+        quantize(v_mx)
+        for j in range(PAIRS):
+            tanh(j)
+            if 2 <= j < 6:
+                deal(nc.scalar.copy, q_mx[2][0][:], q_raw[2][:], 4, slice(32 * (j - 2), 32 * (j - 1)))
+            weigh(j)
+            if j > 0:
+                quantize(w_mx[j - 1])
+            if j == 5:
+                quantize(q_mx[2])
+            if j + 2 < PAIRS:
+                score_matmuls(j + 2)
+            if j >= 11 and j <= 14:
+                value_matmuls(0, j - 11)
+        quantize(w_mx[PAIRS - 1])
+        for g in range(TILES):
+            norm(0, g)
+            finish(0, g)
+            value_matmuls(1, g)
+        for g in range(TILES):
+            norm(1, g)
+            finish(1, g)

@@ -24,7 +24,7 @@ EPS = 1e-5
 
 
 def head_of(s, g):
-    return 4 * (g // 2) + 2 * s + g % 2
+    return 2 + g if s == 0 else (0, 1, 6, 7)[g]
 
 
 def deal(copy, dealt, raw, places, part):
@@ -59,25 +59,17 @@ def tile_rows_a_tanh_onorm_kernel(tc, qT, kT, t, v, gn, out):
         v_raw = sb.tile([P, KV, PACK * D], F32, name="v_raw", align_bytes=64)
         t_sb = sb.tile([P, PACK], F32, name="t_sb", align_bytes=64)
         gn_sb = sb.tile([P, D], F32, name="gn_sb", align_bytes=64)
-        queues = [nc.sync, nc.scalar]
-
-        for dup in range(2):
-            for kv in range(KV):
-                g = 2 * kv + dup
-                queues[kv].dma_start(out=k_raw[ROWS * g : ROWS * (g + 1)], in_=kT[kv].rearrange("(p j) n -> p j n", j=PACK))
-
-        def load_q(i):
-            s, q0, width = chunks[i]
-            for kv in range(KV):
-                h0 = head_of(s, 2 * kv)
-                src = qT[h0 : h0 + 2].rearrange("h (p j) q -> (h p) j q", j=PACK)
-                queues[kv].dma_start(out=q_raw[i][64 * kv : 64 * (kv + 1)], in_=src[:, :, q0 : q0 + width])
-
-        load_q(0)
-        load_q(1)
+        k_rows = kT.rearrange("k (p j) n -> (k p) j n", j=PACK)
+        q_rows = qT.rearrange("h (p j) q -> (h p) j q", j=PACK)
+        nc.sync.dma_start(out=k_raw[96:128], in_=k_rows[32:64])
+        nc.scalar.dma_start(out=k_raw[0:32], in_=k_rows[0:32])
+        nc.sync.dma_start(out=k_raw[32:96], in_=k_rows)
+        nc.sync.dma_start(out=q_raw[0][:], in_=q_rows[64:192, :, 0:256])
         nc.sync.dma_start(out=t_sb[:], in_=t.rearrange("(p r) o -> p (r o)", r=PACK))
+        nc.sync.dma_start(out=q_raw[1][:], in_=q_rows[64:192, :, 256:512])
         nc.sync.dma_start(out=v_raw[:], in_=v.rearrange("k (p r) e -> p k (r e)", r=PACK))
-        load_q(2)
+        nc.sync.dma_start(out=q_raw[2][0:64], in_=q_rows[0:64])
+        nc.sync.dma_start(out=q_raw[2][64:128], in_=q_rows[192:256])
         nc.sync.dma_start(out=gn_sb[:], in_=gn)
 
         k_mx = mx_tiles("k", N)
@@ -162,9 +154,11 @@ def tile_rows_a_tanh_onorm_kernel(tc, qT, kT, t, v, gn, out):
             dst = out[head_of(s, g)].rearrange("(c p r) e -> p c (r e)", c=nchunks, p=P)
             nc.sync.dma_start(out=dst, in_=result[u][:].rearrange("p (c r) e -> p c (r e)", c=nchunks))
 
-        deal(nc.vector.tensor_copy, k_mx[0][:], k_raw[:], 4, slice(0, COLS))
+        deal(nc.vector.tensor_copy, k_mx[0][:], k_raw[:], 4, slice(0, 88))
+        deal(nc.scalar.copy, k_mx[0][:], k_raw[:], 4, slice(88, COLS))
         quantize(k_mx)
-        deal(nc.scalar.copy, q_mx[0][0][:], q_raw[0][:], 2, slice(0, COLS))
+        deal(nc.scalar.copy, q_mx[0][0][:], q_raw[0][:], 2, slice(0, 64))
+        deal(nc.vector.tensor_copy, q_mx[0][0][:], q_raw[0][:], 2, slice(64, COLS))
         quantize(q_mx[0])
         score_matmuls(0)
         score_matmuls(1)
@@ -177,9 +171,11 @@ def tile_rows_a_tanh_onorm_kernel(tc, qT, kT, t, v, gn, out):
         quantize(v_mx)
         for j in range(PAIRS):
             tanh(j)
-            if 2 <= j < 6:
-                deal(nc.scalar.copy, q_mx[2][0][:], q_raw[2][:], 4, slice(32 * (j - 2), 32 * (j - 1)))
+            if j in (3, 4):
+                deal(nc.scalar.copy, q_mx[2][0][:], q_raw[2][:], 4, slice(32 * (j - 3), 32 * (j - 2)))
             weigh(j)
+            if j == 4:
+                deal(nc.vector.tensor_copy, q_mx[2][0][:], q_raw[2][:], 4, slice(64, COLS))
             if j > 0:
                 quantize(w_mx[j - 1])
             if j == 5:

@@ -9,6 +9,7 @@ F32 = mybir.dt.float32
 BF16 = mybir.dt.bfloat16
 U32 = mybir.dt.uint32
 U8 = mybir.dt.uint8
+I32 = mybir.dt.int32
 FP8X4 = mybir.dt.float8_e4m3fn_x4
 ACT = mybir.ActivationFunctionType
 MULT = mybir.AluOpType.mult
@@ -21,6 +22,8 @@ COLS = 128
 SETS = 2
 PAIRS = 16
 EPS = 1e-5
+ORDER = (1, 2, 0, 3)
+UNITS = 32
 
 
 def head_of(s, g):
@@ -52,7 +55,7 @@ def tile_rows_a_tanh_onorm_kernel(tc, qT, kT, t, v, gn, out):
             values, codes, scales = tiles
             nc.vector.quantize_mx(out=codes[:].bitcast(FP8X4), scales=scales[:], in_=values[:])
 
-        chunks = [(0, 0, 256), (0, 256, 256), (1, 0, 512)]
+        chunks = [(0, 0, 256), (0, 256, 256), (1, 0, 256), (1, 256, 256)]
 
         k_raw = sb.tile([P, PACK, N], F32, name="k_raw", align_bytes=64)
         q_raw = [sb.tile([P, PACK, c[2]], F32, name="q_raw%d" % i, align_bytes=64) for i, c in enumerate(chunks)]
@@ -68,11 +71,14 @@ def tile_rows_a_tanh_onorm_kernel(tc, qT, kT, t, v, gn, out):
         nc.sync.dma_start(out=t_sb[:], in_=t.rearrange("(p r) o -> p (r o)", r=PACK))
         nc.sync.dma_start(out=q_raw[1][:], in_=q_rows[64:192, :, 256:512])
         nc.sync.dma_start(out=v_raw[:], in_=v.rearrange("k (p r) e -> p k (r e)", r=PACK))
-        nc.sync.dma_start(out=q_raw[2][0:64], in_=q_rows[0:64])
-        nc.sync.dma_start(out=q_raw[2][64:128], in_=q_rows[192:256])
+        for c in range(2):
+            nc.sync.dma_start(out=q_raw[2 + c][0:64], in_=q_rows[0:64, :, 256 * c : 256 * (c + 1)])
+            nc.sync.dma_start(out=q_raw[2 + c][64:128], in_=q_rows[192:256, :, 256 * c : 256 * (c + 1)])
         nc.sync.dma_start(out=gn_sb[:], in_=gn)
 
         k_mx = mx_tiles("k", N)
+        zero = sb.tile([P, 1], F32, name="zero", align_bytes=64)
+        eps = sb.tile([P, 1], F32, name="eps", align_bytes=64)
         q_mx = [mx_tiles("q%d" % i, c[2]) for i, c in enumerate(chunks)]
         v_mx = mx_tiles("v", KV * D)
         w_mx = [mx_tiles("w%d" % j, 2 * COLS) for j in range(PAIRS)]
@@ -84,31 +90,24 @@ def tile_rows_a_tanh_onorm_kernel(tc, qT, kT, t, v, gn, out):
         squares = [sb.tile([P, PACK * D], F32, name="squares%d" % i, align_bytes=64) for i in range(2)]
         result = [sb.tile([P, PACK, D], F32, name="result%d" % i, align_bytes=64) for i in range(SETS * TILES)]
 
-        def score_matmuls(j):
-            s, tau, half = j // 8, (j % 8) // 2, j % 2
-            if s == 0:
-                codes, scales = q_mx[tau // 2][1:]
-                qc = slice(COLS * (tau % 2), COLS * (tau % 2 + 1))
-            else:
-                codes, scales = q_mx[2][1:]
-                qc = slice(COLS * tau, COLS * (tau + 1))
-            for r in range(PACK):
-                kc = slice(COLS * r, COLS * (r + 1))
-                for g in (2 * half, 2 * half + 1):
-                    rows = slice(ROWS * g, ROWS * (g + 1))
-                    nc.tensor.matmul_mx(
-                        out=scores[g][:, kc],
-                        lhsT=k_mx[1][rows, kc].bitcast(FP8X4), lhsT_scale=k_mx[2][rows, kc],
-                        rhs=codes[rows, qc].bitcast(FP8X4), rhs_scale=scales[rows, qc],
-                        start=True, stop=True,
-                    )
+        def score_matmul(u, r):
+            s, tau, g = u // 16, (u % 16) // 4, ORDER[u % 4]
+            codes, scales = q_mx[2 * s + tau // 2][1:]
+            qc = slice(COLS * (tau % 2), COLS * (tau % 2 + 1))
+            kc = slice(COLS * r, COLS * (r + 1))
+            rows = slice(ROWS * g, ROWS * (g + 1))
+            nc.tensor.matmul_mx(
+                out=scores[g][:, kc],
+                lhsT=k_mx[1][rows, kc].bitcast(FP8X4), lhsT_scale=k_mx[2][rows, kc],
+                rhs=codes[rows, qc].bitcast(FP8X4), rhs_scale=scales[rows, qc],
+                start=True, stop=True,
+            )
 
-        def tanh(j):
-            for i in range(2):
-                g = 2 * (j % 2) + i
-                nc.scalar.activation(
-                    out=p_sb[j][:, i], in_=scores[g][:].rearrange("p (r n) -> p n r", r=PACK), func=ACT.Tanh
-                )
+        def tanh(u):
+            nc.scalar.activation(
+                out=p_sb[u // 2][:, u % 2], in_=scores[ORDER[u % 4]][:].rearrange("p (r n) -> p n r", r=PACK),
+                func=ACT.Tanh,
+            )
 
         def weigh(j):
             nc.vector.tensor_tensor(
@@ -118,29 +117,31 @@ def tile_rows_a_tanh_onorm_kernel(tc, qT, kT, t, v, gn, out):
                 op=MULT,
             )
 
-        def value_matmuls(s, g):
+        def value_matmul(u):
+            tau, g = (u % 16) // 4, ORDER[u % 4]
             vc = slice(D * (g // 2), D * (g // 2 + 1))
-            wc = slice(COLS * (g % 2), COLS * (g % 2 + 1))
-            for tau in range(PACK):
-                codes, scales = w_mx[8 * s + 2 * tau + g // 2][1:]
-                nc.tensor.matmul_mx(
-                    out=y[g][:, D * tau : D * (tau + 1)],
-                    lhsT=codes[:, wc].bitcast(FP8X4), lhsT_scale=scales[:, wc],
-                    rhs=v_mx[1][:, vc].bitcast(FP8X4), rhs_scale=v_mx[2][:, vc],
-                    start=True, stop=True,
-                )
+            wc = slice(COLS * (u % 2), COLS * (u % 2 + 1))
+            codes, scales = w_mx[u // 2][1:]
+            nc.tensor.matmul_mx(
+                out=y[g][:, D * tau : D * (tau + 1)],
+                lhsT=codes[:, wc].bitcast(FP8X4), lhsT_scale=scales[:, wc],
+                rhs=v_mx[1][:, vc].bitcast(FP8X4), rhs_scale=v_mx[2][:, vc],
+                start=True, stop=True,
+            )
 
-        def norm(s, g):
+        def square(s, g, tau):
             u = TILES * s + g
-            for tau in range(PACK):
-                cols = slice(D * tau, D * (tau + 1))
-                nc.scalar.activation(
-                    out=squares[u % 2][:, cols], in_=y[g][:, cols], func=ACT.Square, scale=1.0 / 16,
-                    accum_out=ssq[:, u, tau : tau + 1],
-                )
+            cols = slice(D * tau, D * (tau + 1))
+            nc.scalar.activation(
+                out=squares[u % 2][:, cols], in_=y[g][:, cols], func=ACT.Square, scale=1.0 / 16,
+                accum_out=ssq[:, u, tau : tau + 1],
+            )
+
+        def root(s, g):
+            u = TILES * s + g
             nc.scalar.activation(
                 out=rstd[:, u, 0:PACK], in_=ssq[:, u, 0:PACK], func=ACT.Abs_reciprocal_sqrt,
-                scale=256.0 / D, bias=256.0 * EPS,
+                scale=256.0 / D, bias=eps[:],
             )
 
         def finish(s, g):
@@ -150,18 +151,21 @@ def tile_rows_a_tanh_onorm_kernel(tc, qT, kT, t, v, gn, out):
                     out=result[u][:, tau], in0=y[g][:, D * tau : D * (tau + 1)], scalar=rstd[:, u, tau : tau + 1],
                     in1=gn_sb[:], op0=MULT, op1=MULT,
                 )
-            nchunks = 2 if s == 0 else 1
+            nchunks = 2
             dst = out[head_of(s, g)].rearrange("(c p r) e -> p c (r e)", c=nchunks, p=P)
             nc.sync.dma_start(out=dst, in_=result[u][:].rearrange("p (c r) e -> p c (r e)", c=nchunks))
 
+        nc.vector.memset(zero[:], 0.0)
+        nc.scalar.activation(out=eps[:], in_=zero[:], func=ACT.Copy, bias=256.0 * EPS)
         deal(nc.vector.tensor_copy, k_mx[0][:], k_raw[:], 4, slice(0, 88))
         deal(nc.scalar.copy, k_mx[0][:], k_raw[:], 4, slice(88, COLS))
         quantize(k_mx)
-        deal(nc.scalar.copy, q_mx[0][0][:], q_raw[0][:], 2, slice(0, 64))
-        deal(nc.vector.tensor_copy, q_mx[0][0][:], q_raw[0][:], 2, slice(64, COLS))
+        deal(nc.scalar.copy, q_mx[0][0][:], q_raw[0][:], 2, slice(88, COLS))
+        deal(nc.vector.tensor_copy, q_mx[0][0][:], q_raw[0][:], 2, slice(0, 88))
         quantize(q_mx[0])
-        score_matmuls(0)
-        score_matmuls(1)
+        for r in range(PACK):
+            for u in range(TILES):
+                score_matmul(u, r)
         deal(nc.vector.tensor_copy, q_mx[1][0][:], q_raw[1][:], 2, slice(0, COLS))
         nc.vector.tensor_copy(
             out=v_mx[0][:].rearrange("p (k c i r) -> p k c r i", k=KV, i=4, r=PACK),
@@ -169,26 +173,48 @@ def tile_rows_a_tanh_onorm_kernel(tc, qT, kT, t, v, gn, out):
         )
         quantize(q_mx[1])
         quantize(v_mx)
-        for j in range(PAIRS):
-            tanh(j)
-            if j in (3, 4):
-                deal(nc.scalar.copy, q_mx[2][0][:], q_raw[2][:], 4, slice(32 * (j - 3), 32 * (j - 2)))
-            weigh(j)
-            if j == 4:
-                deal(nc.vector.tensor_copy, q_mx[2][0][:], q_raw[2][:], 4, slice(64, COLS))
-            if j > 0:
-                quantize(w_mx[j - 1])
-            if j == 5:
-                quantize(q_mx[2])
-            if j + 2 < PAIRS:
-                score_matmuls(j + 2)
-            if j >= 11 and j <= 14:
-                value_matmuls(0, j - 11)
-        quantize(w_mx[PAIRS - 1])
-        for g in range(TILES):
-            norm(0, g)
-            finish(0, g)
-            value_matmuls(1, g)
-        for g in range(TILES):
-            norm(1, g)
-            finish(1, g)
+        for u in range(UNITS):
+            tanh(u)
+            if u in (9, 10):
+                deal(nc.scalar.copy, q_mx[2][0][:], q_raw[2][:], 2, slice(64 * (u - 9), 64 * (u - 8)))
+            if u == 14:
+                deal(nc.scalar.copy, q_mx[3][0][:], q_raw[3][:], 2, slice(0, 64))
+            if u % 2 == 1 and u < UNITS - 1:
+                if u == 11:
+                    quantize(q_mx[2])
+                if u == 17:
+                    quantize(q_mx[3])
+                weigh(u // 2)
+                if u == 13:
+                    deal(nc.vector.tensor_copy, q_mx[3][0][:], q_raw[3][:], 2, slice(64, COLS))
+                if u > 1:
+                    quantize(w_mx[u // 2 - 1])
+            for r in range(2):
+                if u + 4 < UNITS:
+                    score_matmul(u + 4, r)
+                if 1 <= u and u + 3 < UNITS:
+                    score_matmul(u + 3, r + 2)
+            if u == UNITS - 4:
+                for i in range(TILES):
+                    for tau in range(PACK):
+                        value_matmul(4 * tau + i)
+        heads = [(s, g) for s in range(SETS) for g in ORDER]
+        for tau in range(PACK):
+            square(0, ORDER[0], tau)
+        for i, (s, g) in enumerate(heads):
+            follows = heads[i + 1] if i + 1 < len(heads) else None
+            if follows:
+                square(follows[0], follows[1], 0)
+            root(s, g)
+            finish(s, g)
+            if i == 0:
+                weigh(PAIRS - 1)
+                quantize(w_mx[PAIRS - 2])
+            if i == 1:
+                quantize(w_mx[PAIRS - 1])
+            if s == 0:
+                for tau in range(PACK):
+                    value_matmul(16 + 4 * tau + i)
+            if follows:
+                for tau in range(1, PACK):
+                    square(follows[0], follows[1], tau)

from contextlib import ExitStack

import concourse.mybir as mybir

H, KV, D, NQ, N = 8, 2, 128, 512, 512
FLOPS = 2 * 2 * H * NQ * N * D

F32 = mybir.dt.float32
BF16 = mybir.dt.bfloat16
U32 = mybir.dt.uint32
U8 = mybir.dt.uint8
I32 = mybir.dt.int32
FP8X4 = mybir.dt.float8_e4m3fn_x4
ACT = mybir.ActivationFunctionType
MULT = mybir.AluOpType.mult

P = 128
PACK = 4
ROWS = 32
TILES = 4
COLS = 128
SETS = 2
PAIRS = 16
EPS = 1e-5
ORDER = (1, 2, 0, 3)
UNITS = 32


def head_of(s, g):
    return 2 + g if s == 0 else (0, 1, 6, 7)[g]


def deal(copy, dealt, raw, places, part):
    run = PACK // places
    src = raw.rearrange("p j (a b r) -> p a j b r", b=run, r=places)
    dst = dealt.rearrange("p (r a b j) -> p a j b r", r=places, b=run, j=PACK)
    rows = slice(part.start // run, part.stop // run)
    copy(out=dst[:, rows], in_=src[:, rows])


def tile_rows_a_tanh_onorm_kernel(tc, qT, kT, t, v, gn, out):
    nc = tc.nc
    with ExitStack() as ctx:
        sb = ctx.enter_context(tc.tile_pool(name="sb", bufs=1))
        ps = ctx.enter_context(tc.psum_pool(name="ps", bufs=1))
        ctx.enter_context(tc.manual_schedule())

        def mx_tiles(name, words):
            values = sb.tile([P, PACK * words], BF16, name=name + "_bf", align_bytes=64)
            codes = sb.tile([P, words], U32, name=name + "_codes", align_bytes=64)
            scales = sb.tile([P, words], U8, name=name + "_scales", align_bytes=64)
            return values, codes, scales

        def quantize(tiles):
            values, codes, scales = tiles
            nc.vector.quantize_mx(out=codes[:].bitcast(FP8X4), scales=scales[:], in_=values[:])

        chunks = [(0, 0, 256), (0, 256, 256), (1, 0, 256), (1, 256, 256)]

        k_raw = sb.tile([P, PACK, N], F32, name="k_raw", align_bytes=64)
        q_raw = [sb.tile([P, PACK, c[2]], F32, name="q_raw%d" % i, align_bytes=64) for i, c in enumerate(chunks)]
        v_raw = sb.tile([P, KV, PACK * D], F32, name="v_raw", align_bytes=64)
        t_sb = sb.tile([P, PACK], F32, name="t_sb", align_bytes=64)
        gn_sb = sb.tile([P, D], F32, name="gn_sb", align_bytes=64)
        k_rows = kT.rearrange("k (p j) n -> (k p) j n", j=PACK)
        q_rows = qT.rearrange("h (p j) q -> (h p) j q", j=PACK)
        nc.sync.dma_start(out=k_raw[96:128], in_=k_rows[32:64])
        nc.scalar.dma_start(out=k_raw[0:32], in_=k_rows[0:32])
        nc.sync.dma_start(out=k_raw[32:96], in_=k_rows)
        nc.sync.dma_start(out=q_raw[0][:], in_=q_rows[64:192, :, 0:256])
        nc.sync.dma_start(out=t_sb[:], in_=t.rearrange("(p r) o -> p (r o)", r=PACK))
        nc.sync.dma_start(out=q_raw[1][:], in_=q_rows[64:192, :, 256:512])
        nc.sync.dma_start(out=v_raw[:], in_=v.rearrange("k (p r) e -> p k (r e)", r=PACK))
        for c in range(2):
            nc.sync.dma_start(out=q_raw[2 + c][0:64], in_=q_rows[0:64, :, 256 * c : 256 * (c + 1)])
            nc.sync.dma_start(out=q_raw[2 + c][64:128], in_=q_rows[192:256, :, 256 * c : 256 * (c + 1)])
        nc.sync.dma_start(out=gn_sb[:], in_=gn)

        k_mx = mx_tiles("k", N)
        zero = sb.tile([P, 1], F32, name="zero", align_bytes=64)
        eps = sb.tile([P, 1], F32, name="eps", align_bytes=64)
        q_mx = [mx_tiles("q%d" % i, c[2]) for i, c in enumerate(chunks)]
        v_mx = mx_tiles("v", KV * D)
        w_mx = [mx_tiles("w%d" % j, 2 * COLS) for j in range(PAIRS)]
        p_sb = [sb.tile([P, 2, COLS, PACK], F32, name="p%d" % j, align_bytes=64) for j in range(PAIRS)]
        scores = [ps.tile([P, PACK * COLS], F32, name="scores%d" % g) for g in range(TILES)]
        y = [ps.tile([P, PACK * D], F32, name="y%d" % g) for g in range(TILES)]
        ssq = sb.tile([P, SETS * TILES, 8], F32, name="ssq", align_bytes=64)
        rstd = sb.tile([P, SETS * TILES, 8], F32, name="rstd", align_bytes=64)
        squares = [sb.tile([P, PACK * D], F32, name="squares%d" % i, align_bytes=64) for i in range(2)]
        result = [sb.tile([P, PACK, D], F32, name="result%d" % i, align_bytes=64) for i in range(SETS * TILES)]

        def score_matmul(u, r):
            s, tau, g = u // 16, (u % 16) // 4, ORDER[u % 4]
            codes, scales = q_mx[2 * s + tau // 2][1:]
            qc = slice(COLS * (tau % 2), COLS * (tau % 2 + 1))
            kc = slice(COLS * r, COLS * (r + 1))
            rows = slice(ROWS * g, ROWS * (g + 1))
            nc.tensor.matmul_mx(
                out=scores[g][:, kc],
                lhsT=k_mx[1][rows, kc].bitcast(FP8X4), lhsT_scale=k_mx[2][rows, kc],
                rhs=codes[rows, qc].bitcast(FP8X4), rhs_scale=scales[rows, qc],
                start=True, stop=True,
            )

        def tanh(u):
            nc.scalar.activation(
                out=p_sb[u // 2][:, u % 2], in_=scores[ORDER[u % 4]][:].rearrange("p (r n) -> p n r", r=PACK),
                func=ACT.Tanh,
            )

        def weigh(j):
            nc.vector.tensor_tensor(
                out=w_mx[j][0][:].rearrange("p (n r) -> p n r", r=PACK),
                in0=p_sb[j][:].rearrange("p i n r -> p (i n) r"),
                in1=t_sb[:].unsqueeze(1).to_broadcast([P, 2 * COLS, PACK]),
                op=MULT,
            )

        def value_matmul(u):
            tau, g = (u % 16) // 4, ORDER[u % 4]
            vc = slice(D * (g // 2), D * (g // 2 + 1))
            wc = slice(COLS * (u % 2), COLS * (u % 2 + 1))
            codes, scales = w_mx[u // 2][1:]
            nc.tensor.matmul_mx(
                out=y[g][:, D * tau : D * (tau + 1)],
                lhsT=codes[:, wc].bitcast(FP8X4), lhsT_scale=scales[:, wc],
                rhs=v_mx[1][:, vc].bitcast(FP8X4), rhs_scale=v_mx[2][:, vc],
                start=True, stop=True,
            )

        def square(s, g, tau):
            u = TILES * s + g
            cols = slice(D * tau, D * (tau + 1))
            nc.scalar.activation(
                out=squares[u % 2][:, cols], in_=y[g][:, cols], func=ACT.Square, scale=1.0 / 16,
                accum_out=ssq[:, u, tau : tau + 1],
            )

        def root(s, g):
            u = TILES * s + g
            nc.scalar.activation(
                out=rstd[:, u, 0:PACK], in_=ssq[:, u, 0:PACK], func=ACT.Abs_reciprocal_sqrt,
                scale=256.0 / D, bias=eps[:],
            )

        def finish(s, g):
            u = TILES * s + g
            for tau in range(PACK):
                nc.vector.scalar_tensor_tensor(
                    out=result[u][:, tau], in0=y[g][:, D * tau : D * (tau + 1)], scalar=rstd[:, u, tau : tau + 1],
                    in1=gn_sb[:], op0=MULT, op1=MULT,
                )
            nchunks = 2
            dst = out[head_of(s, g)].rearrange("(c p r) e -> p c (r e)", c=nchunks, p=P)
            nc.sync.dma_start(out=dst, in_=result[u][:].rearrange("p (c r) e -> p c (r e)", c=nchunks))

        nc.vector.memset(zero[:], 0.0)
        nc.scalar.activation(out=eps[:], in_=zero[:], func=ACT.Copy, bias=256.0 * EPS)
        deal(nc.vector.tensor_copy, k_mx[0][:], k_raw[:], 4, slice(0, 88))
        deal(nc.scalar.copy, k_mx[0][:], k_raw[:], 4, slice(88, COLS))
        quantize(k_mx)
        deal(nc.scalar.copy, q_mx[0][0][:], q_raw[0][:], 2, slice(88, COLS))
        deal(nc.vector.tensor_copy, q_mx[0][0][:], q_raw[0][:], 2, slice(0, 88))
        quantize(q_mx[0])
        for r in range(PACK):
            for u in range(TILES):
                score_matmul(u, r)
        deal(nc.vector.tensor_copy, q_mx[1][0][:], q_raw[1][:], 2, slice(0, COLS))
        nc.vector.tensor_copy(
            out=v_mx[0][:].rearrange("p (k c i r) -> p k c r i", k=KV, i=4, r=PACK),
            in_=v_raw[:].rearrange("p k (r c i) -> p k c r i", r=PACK, i=4),
        )
        quantize(q_mx[1])
        quantize(v_mx)
        for u in range(UNITS):
            tanh(u)
            if u in (9, 10):
                deal(nc.scalar.copy, q_mx[2][0][:], q_raw[2][:], 2, slice(64 * (u - 9), 64 * (u - 8)))
            if u == 14:
                deal(nc.scalar.copy, q_mx[3][0][:], q_raw[3][:], 2, slice(0, 64))
            if u % 2 == 1 and u < UNITS - 1:
                if u == 11:
                    quantize(q_mx[2])
                if u == 17:
                    quantize(q_mx[3])
                weigh(u // 2)
                if u == 13:
                    deal(nc.vector.tensor_copy, q_mx[3][0][:], q_raw[3][:], 2, slice(64, COLS))
                if u > 1:
                    quantize(w_mx[u // 2 - 1])
            for r in range(2):
                if u + 4 < UNITS:
                    score_matmul(u + 4, r)
                if 1 <= u and u + 3 < UNITS:
                    score_matmul(u + 3, r + 2)
            if u == UNITS - 4:
                for i in range(TILES):
                    for tau in range(PACK):
                        value_matmul(4 * tau + i)
        heads = [(s, g) for s in range(SETS) for g in ORDER]
        for tau in range(PACK):
            square(0, ORDER[0], tau)
        for i, (s, g) in enumerate(heads):
            follows = heads[i + 1] if i + 1 < len(heads) else None
            if follows:
                square(follows[0], follows[1], 0)
            root(s, g)
            finish(s, g)
            if i == 0:
                weigh(PAIRS - 1)
                quantize(w_mx[PAIRS - 2])
            if i == 1:
                quantize(w_mx[PAIRS - 1])
            if s == 0:
                for tau in range(PACK):
                    value_matmul(16 + 4 * tau + i)
            if follows:
                for tau in range(1, PACK):
                    square(follows[0], follows[1], tau)
